import numpy as np
import ml_dtypes


def mxq(x, axis, fmt="e4m3"):
    dtype, down = {"e4m3": (ml_dtypes.float8_e4m3fn, 7), "e5m2": (ml_dtypes.float8_e5m2, 14)}[fmt]
    v = np.moveaxis(np.asarray(x, np.float32).astype(ml_dtypes.bfloat16).astype(np.float64), axis, -1)
    blocks = v.reshape(v.shape[:-1] + (-1, 32))
    amax = np.abs(blocks).max(-1, keepdims=True)
    byte = np.maximum(np.where(amax > 0, np.frexp(amax)[1] - 1 + 127, 0) - down, 1)
    scale = np.exp2(byte - 127.0)
    codes = (blocks / scale).astype(np.float32).astype(dtype).astype(np.float64)
    return np.moveaxis((codes * scale).reshape(v.shape), -1, axis)


WIDE = False


def mx_kscale(k):
    if not WIDE:
        return np.ones(k)
    levels = np.array([10, -10, 5, -5, 0])
    if k % 512:
        return np.exp2(np.random.permutation(np.resize(levels, k // 32))).repeat(32)
    a = np.empty((k // 512, 16))
    for p in range(k // 512):
        a[p, :8] = np.random.permutation(np.resize(levels, 8))
        for g in range(8):
            far = levels[np.abs(levels - a[p, g]) >= 10]
            a[p, g + 8] = far[np.random.randint(len(far))]
    return np.exp2(a.ravel()).repeat(32)


BF16 = ml_dtypes.bfloat16


def bf(x):
    return np.asarray(x, np.float32).astype(BF16)


def f64(x):
    return np.asarray(x).astype(np.float64)


E2M1 = np.array([0.0, 0.5, 1.0, 1.5, 2.0, 3.0, 4.0, 6.0, -0.0, -0.5, -1.0, -1.5, -2.0, -3.0, -4.0, -6.0])


def pack_weight(w, fmt):
    k, n = w.shape
    w = f64(bf(w)).reshape(k // 32, 32, n)
    amax = np.abs(w).max(1)
    if fmt == "e4m3":
        byte = np.frexp(amax)[1] - 1 + 127 - 7
    else:
        mant, ex = np.frexp(amax / 6.0)
        byte = np.where(mant > 0.5, ex, ex - 1) + 127
    byte = np.clip(np.where(amax > 0, byte, 1), 1, 254)
    scaled = (w * np.exp2(127.0 - byte)[:, None, :]).reshape(k, n).astype(np.float32)
    by_word = np.ascontiguousarray(scaled.reshape(k // 512, 128, 4, n).transpose(0, 1, 3, 2))
    if fmt == "e4m3":
        words = by_word.astype(ml_dtypes.float8_e4m3fn).view(np.uint8)
    else:
        c = by_word.astype(ml_dtypes.float4_e2m1fn).view(np.uint8) & 0xF
        words = c[..., 0::2] | (c[..., 1::2] << 4)
    return np.ascontiguousarray(words), np.ascontiguousarray(byte.astype(np.uint8).reshape(k // 512, 16, n))


def unpack_weight(words, scales, fmt):
    g, p, n, _ = words.shape
    if fmt == "e4m3":
        vals = np.ascontiguousarray(words).view(ml_dtypes.float8_e4m3fn).astype(np.float64)
    else:
        nib = np.empty((g, p, n, 4), np.uint8)
        nib[..., 0::2] = words & 0xF
        nib[..., 1::2] = words >> 4
        vals = E2M1[nib]
    vals = vals * np.repeat(np.exp2(scales.astype(np.float64) - 127.0), 8, axis=1)[..., None]
    return vals.transpose(0, 1, 3, 2).reshape(g * 512, n)
def pack4(w):
    words, scales = pack_weight(w, "e2m1")
    return words.reshape(words.shape[0], 128, -1), scales


def unpack4(words, scales):
    return unpack_weight(words.reshape(words.shape[0], 128, -1, 2), scales, "e2m1")


M, K, F, R = 1024, 2048, 1024, 2048


def setup_inputs():
    s, t = mx_kscale(K), mx_kscale(F)
    cells = np.random.standard_normal((K, M)) * s[:, None]
    inter = np.random.standard_normal((K, F)) / np.sqrt(K) / s[:, None] * t
    c_words, c_scales = pack4(cells)
    b_words, b_scales = pack4(inter)
    return {"c_words": c_words,
            "c_scales": c_scales,
            "b_words": b_words,
            "b_scales": b_scales,
            "activity": bf(1.0 + 0.5 * np.random.standard_normal((M, F))),
            "pairs": bf(1.5 * np.random.standard_normal((R, F)) / np.sqrt(F) / t),
            "pair_bias": bf(0.5 * np.random.standard_normal(R))}


def reference(c_words, c_scales, b_words, b_scales, activity, pairs, pair_bias):
    c = unpack4(c_words, c_scales)
    b = unpack4(b_words, b_scales)
    h = c.T @ b
    h = h * f64(activity)
    d = mxq(f64(pairs), 1, "e4m3")
    z = mxq(h, 1, "e4m3") @ d.T
    z = z + f64(pair_bias)
    return 1.0 / (1.0 + np.exp(-z))

@@ -1,0 +1,318 @@
+from contextlib import ExitStack
+
+import concourse.mybir as mybir
+from concourse.masks import make_identity
+
+M, K, F, R = 1024, 2048, 1024, 2048
+FLOPS = 2 * M * K * F + 2 * M * F * R
+
+F32 = mybir.dt.float32
+BF16 = mybir.dt.bfloat16
+I32 = mybir.dt.int32
+U32 = mybir.dt.uint32
+U8 = mybir.dt.uint8
+FP4X4 = mybir.dt.float4_e2m1fn_x4
+FP8X4 = mybir.dt.float8_e4m3fn_x4
+ACT = mybir.ActivationFunctionType
+ALU = mybir.AluOpType
+
+P = 128
+KG = K // 512
+FG = F // 512
+MT = M // P
+RT = R // P
+RC = R // 512
+
+
+def tile_drug_synergy_bilinear_s4_kernel(
+    tc, c_words, c_scales, b_words, b_scales, activity, pairs, pair_bias, out
+):
+    nc = tc.nc
+    with ExitStack() as ctx:
+        keep = ctx.enter_context(tc.tile_pool(name="keep", bufs=1))
+        work = ctx.enter_context(tc.tile_pool(name="work", bufs=3))
+        psum = ctx.enter_context(tc.psum_pool(name="psum", bufs=8))
+        ctx.enter_context(tc.manual_schedule())
+
+        def fixed(name, shape, dtype):
+            return keep.tile(shape, dtype, name=name, tag=name, align_bytes=64)
+
+        def new_bank():
+            return psum.tile([P, 512], F32, name="bank", tag="bank")
+
+        c_plane = fixed("c_plane", [P, KG * M], U8)
+        b_plane = fixed("b_plane", [P, KG * F], U8)
+        c_code = [fixed("c_code%d" % g, [P, 2 * M], U8) for g in range(KG)]
+        b_code = [fixed("b_code%d" % g, [P, 2 * F], U8) for g in range(KG)]
+        act = [fixed("act%d" % j, [P, 2, F], BF16) for j in range(MT // 2)]
+        raw = [fixed("raw%d" % j, [P, 2, F], BF16) for j in range(RT // 2)]
+        d_code = fixed("d_code", [P, FG, R], U32)
+        d_plane = fixed("d_plane", [P, FG, R], U8)
+        ident = fixed("ident", [P, P], F32)
+        bias_rows = fixed("bias_rows", [P, 256], BF16)
+        bias_cols = fixed("bias_cols", [P, 8], F32)
+        bias = fixed("bias", [P, R], BF16)
+        warm = fixed("warm", [P, 1], F32)
+
+        nc.vector.memset(c_plane[:].bitcast(I32), 0)
+        nc.vector.memset(bias_rows[:].bitcast(I32), 0)
+        nc.vector.memset(b_plane[:].bitcast(I32), 0)
+        nc.vector.memset(warm[:], 0.0)
+        pairs_v = pairs.rearrange("(n i p) k -> n p i k", i=2, p=P)
+        act_v = activity.rearrange("(n i p) f -> n p i f", i=2, p=P)
+        c_scales_v = c_scales.bitcast(I32).rearrange("g r n -> r g n")
+        b_scales_v = b_scales.bitcast(I32).rearrange("g r n -> r g n")
+
+        def load_pairs(j, queue=nc.sync):
+            queue.dma_start(out=raw[j][:], in_=pairs_v[j])
+
+        def load_act(j):
+            nc.sync.dma_start(out=act[j][:], in_=act_v[j])
+
+        def load_codes(g, queue):
+            queue.dma_start(out=c_code[g][:].bitcast(I32), in_=c_words[g].bitcast(I32))
+            queue.dma_start(out=b_code[g][:].bitcast(I32), in_=b_words[g].bitcast(I32))
+
+        def load_scales(queue, plane, source, q):
+            queue.dma_start(
+                out=plane[32 * q : 32 * q + 4, :].bitcast(I32).rearrange("p (g n) -> p g n", g=KG),
+                in_=source[4 * q : 4 * q + 4],
+            )
+
+        load_pairs(0, nc.gpsimd)
+        make_identity(nc, ident[:])
+        load_pairs(1, nc.gpsimd)
+        for q in range(4):
+            load_scales(nc.sync, c_plane, c_scales_v, q)
+            load_scales(nc.scalar, b_plane, b_scales_v, q)
+        load_codes(0, nc.gpsimd)
+        nc.gpsimd.dma_start(out=bias_rows[0:8, :], in_=pair_bias.rearrange("(c n) -> c n", n=256))
+        for g in range(1, KG):
+            load_codes(g, nc.sync)
+        load_act(0)
+        load_act(1)
+        load_pairs(2)
+        load_pairs(3)
+        load_act(2)
+        load_pairs(4)
+        load_pairs(5)
+        load_pairs(6)
+        load_act(3)
+        load_pairs(7)
+        nc.scalar.activation(out=warm[:], in_=warm[:], func=ACT.Sigmoid)
+
+        def bias_step():
+            bank = new_bank()
+            nc.tensor.transpose(bank[:, 0:P], bias_rows[:].bitcast(F32), ident[:])
+            nc.scalar.copy(out=bias_cols[:], in_=bank[:, 0:8])
+            for half in range(2):
+                bank = new_bank()
+                for i in range(4):
+                    c = 4 * half + i
+                    nc.tensor.transpose(
+                        bank[:, i * P : (i + 1) * P], bias_cols[:, c : c + 1].to_broadcast([P, P]), ident[:]
+                    )
+                nc.scalar.copy(out=bias[:, 1024 * half : 1024 * (half + 1)].bitcast(F32), in_=bank[:])
+
+        perm = {}
+        grouped = {}
+
+        def pairs_permute(j, copy=nc.vector.tensor_copy):
+            t = work.tile([P, 2 * F // 2], F32, name="perm", tag="perm", bufs=4, align_bytes=64)
+            perm[j] = t
+            copy(
+                out=t[:].rearrange("p (u n x) -> p u n x", u=2, x=8),
+                in_=raw[j][:].rearrange("p i k -> p (i k)").bitcast(F32).rearrange("p (n u x) -> p u n x", u=2, x=8),
+            )
+
+        def pairs_turn(i):
+            j, rc = i // 2, i // 4
+            if i % 4 == 0:
+                grouped[rc] = work.tile([P, FG, 512, 4], BF16, name="grouped", tag="grouped", bufs=2, align_bytes=64)
+            bank = new_bank()
+            words = perm[j][:]
+            for g in range(FG):
+                for u in range(2):
+                    start = 512 * u + 256 * (i % 2) + 128 * g
+                    nc.tensor.transpose(
+                        bank[:, (2 * g + u) * P : (2 * g + u + 1) * P], words[:, start : start + P], ident[:]
+                    )
+            r0 = 128 * (i % 4)
+            nc.scalar.copy(
+                out=grouped[rc][:].rearrange("p g r t -> p g (r t)").bitcast(F32)[:, :, 2 * r0 : 2 * r0 + 256].rearrange("p g (r u) -> p g r u", u=2),
+                in_=bank[:].rearrange("p (g u r) -> p g r u", g=FG, u=2),
+            )
+
+        def pairs_quantize(rc, g):
+            cols = slice(512 * rc, 512 * (rc + 1))
+            nc.vector.quantize_mx(
+                out=d_code[:, g, cols].bitcast(FP8X4),
+                scales=d_plane[:, g, cols],
+                in_=grouped[rc][:, g].rearrange("p r t -> p (r t)"),
+            )
+
+        def first_pass(bank, m, f, g):
+            nc.tensor.matmul_mx(
+                out=bank[:],
+                lhsT=c_code[g][:, 256 * m : 256 * (m + 1)].bitcast(FP4X4),
+                lhsT_scale=c_plane[:, M * g + P * m : M * g + P * (m + 1)],
+                rhs=b_code[g][:, 1024 * f : 1024 * (f + 1)].bitcast(FP4X4),
+                rhs_scale=b_plane[:, F * g + 512 * f : F * g + 512 * (f + 1)],
+                start=(g == 0),
+                stop=(g == KG - 1),
+            )
+
+        gated = {}
+        h_code = {}
+        h_plane = {}
+        h_turned = {}
+
+        def gate(bank, m, f):
+            if f == 0:
+                gated[m] = work.tile([P, F], BF16, name="gated", tag="gated", bufs=4, align_bytes=64)
+            nc.vector.tensor_tensor(
+                out=gated[m][:].rearrange("p (u g n) -> p u g n", u=2, g=FG)[:, :, f, :].rearrange("p u (b x) -> p u b x", x=16),
+                in0=bank[:].rearrange("p (b u x) -> p u b x", u=2, x=16),
+                in1=act[m // 2][:, m % 2, 512 * f : 512 * (f + 1)].rearrange("p (b u x) -> p u b x", u=2, x=16),
+                op=ALU.mult,
+            )
+
+        def first(m):
+            for f in range(2):
+                bank = new_bank()
+                for g in range(KG):
+                    first_pass(bank, m, f, g)
+                gate(bank, m, f)
+
+        def first_pair(ms):
+            banks = {}
+            for m in ms:
+                for f in range(2):
+                    banks[(m, f)] = new_bank()
+            for g in range(KG):
+                for m in ms:
+                    for f in range(2):
+                        first_pass(banks[(m, f)], m, f, g)
+            for m in ms:
+                for f in range(2):
+                    gate(banks[(m, f)], m, f)
+
+        def h_turn(m):
+            bank = new_bank()
+            words = gated[m][:].bitcast(F32)
+            for g in range(FG):
+                for u in range(2):
+                    start = 256 * u + 128 * g
+                    nc.tensor.transpose(
+                        bank[:, (2 * g + u) * P : (2 * g + u + 1) * P], words[:, start : start + P], ident[:]
+                    )
+            h_turned[m] = work.tile([P, 4 * FG * P], BF16, name="h_turned", tag="h_turned", bufs=4, align_bytes=64)
+            nc.scalar.copy(
+                out=h_turned[m][:].bitcast(F32).rearrange("p (g r u) -> p g r u", g=FG, u=2),
+                in_=bank[:].rearrange("p (g u r) -> p g r u", g=FG, u=2),
+            )
+
+        def h_quantize(m):
+            h_code[m] = work.tile([P, FG * P], U32, name="h_code", tag="h_code", bufs=4, align_bytes=64)
+            h_plane[m] = work.tile([P, FG * P], U8, name="h_plane", tag="h_plane", bufs=4, align_bytes=64)
+            nc.vector.quantize_mx(out=h_code[m][:].bitcast(FP8X4), scales=h_plane[m][:], in_=h_turned[m][:])
+
+        def second(m, half, fine=False):
+            z = work.tile([P, 1024], F32, name="z", tag="z", bufs=6, align_bytes=64)
+            for i in range(2):
+                rc = 2 * half + i
+                bank = new_bank()
+                cols = slice(512 * rc, 512 * (rc + 1))
+                for g in range(FG):
+                    nc.tensor.matmul_mx(
+                        out=bank[:],
+                        lhsT=h_code[m][:, P * g : P * (g + 1)].bitcast(FP8X4),
+                        lhsT_scale=h_plane[m][:, P * g : P * (g + 1)],
+                        rhs=d_code[:, g, cols].bitcast(FP8X4),
+                        rhs_scale=d_plane[:, g, cols],
+                        start=(g == 0),
+                        stop=(g == FG - 1),
+                    )
+                nc.vector.tensor_tensor(
+                    out=z[:, 512 * i : 512 * (i + 1)], in0=bank[:], in1=bias[:, cols], op=ALU.add
+                )
+                if fine:
+                    part = slice(512 * i, 512 * (i + 1))
+                    nc.scalar.activation(out=z[:, part], in_=z[:, part], func=ACT.Sigmoid)
+                    nc.sync.dma_start(out=out[P * m : P * (m + 1), cols], in_=z[:, part])
+            if not fine:
+                nc.scalar.activation(out=z[:], in_=z[:], func=ACT.Sigmoid)
+                nc.sync.dma_start(out=out[P * m : P * (m + 1), 1024 * half : 1024 * (half + 1)], in_=z[:])
+
+        pairs_permute(0)
+        pairs_turn(0)
+        pairs_turn(1)
+        pairs_permute(1)
+        pairs_turn(2)
+        pairs_turn(3)
+        first_pair((0, 1))
+        first(2)
+        bias_step()
+        pairs_permute(2)
+        pairs_permute(3)
+        h_turn(0)
+        h_turn(1)
+        h_turn(2)
+        pairs_quantize(0, 0)
+        pairs_quantize(0, 1)
+        pairs_turn(4)
+        pairs_turn(5)
+        first(3)
+        pairs_permute(4, nc.scalar.copy)
+        pairs_permute(5, nc.scalar.copy)
+        first(4)
+        pairs_turn(6)
+        pairs_turn(7)
+        pairs_permute(6)
+        pairs_permute(7)
+        pairs_quantize(1, 0)
+        pairs_quantize(1, 1)
+        h_quantize(0)
+        h_quantize(1)
+        pairs_turn(8)
+        pairs_turn(9)
+        pairs_turn(10)
+        pairs_turn(11)
+        pairs_turn(12)
+        pairs_turn(13)
+        pairs_quantize(2, 0)
+        pairs_quantize(2, 1)
+        pairs_turn(14)
+        pairs_turn(15)
+        h_quantize(2)
+        h_turn(3)
+        h_turn(4)
+        second(0, 0)
+        first(5)
+        pairs_quantize(3, 0)
+        pairs_quantize(3, 1)
+        second(1, 0)
+        first(6)
+        second(0, 1)
+        second(1, 1)
+        h_quantize(3)
+        h_turn(5)
+        h_turn(6)
+        h_quantize(4)
+        second(2, 0)
+        second(2, 1)
+        h_quantize(5)
+        second(3, 0)
+        second(3, 1)
+        second(4, 0)
+        first(7)
+        second(4, 1)
+        h_quantize(6)
+        h_turn(7)
+        second(5, 0)
+        second(5, 1)
+        second(6, 0)
+        h_quantize(7)
+        second(6, 1)
+        second(7, 0)
+        second(7, 1, fine=True)

@@ -49,13 +49,10 @@ def tile_drug_synergy_bilinear_s4_kernel(
         d_code = fixed("d_code", [P, FG, R], U32)
         d_plane = fixed("d_plane", [P, FG, R], U8)
         ident = fixed("ident", [P, P], F32)
-        bias_rows = fixed("bias_rows", [P, 256], BF16)
-        bias_cols = fixed("bias_cols", [P, 8], F32)
         bias = fixed("bias", [P, R], BF16)
         warm = fixed("warm", [P, 1], F32)
 
         nc.vector.memset(c_plane[:].bitcast(I32), 0)
-        nc.vector.memset(bias_rows[:].bitcast(I32), 0)
         nc.vector.memset(b_plane[:].bitcast(I32), 0)
         nc.vector.memset(warm[:], 0.0)
         pairs_v = pairs.rearrange("(n i p) k -> n p i k", i=2, p=P)
@@ -79,40 +76,29 @@ def tile_drug_synergy_bilinear_s4_kernel(
                 in_=source[4 * q : 4 * q + 4],
             )
 
-        load_pairs(0, nc.gpsimd)
         make_identity(nc, ident[:])
-        load_pairs(1, nc.gpsimd)
+        load_codes(0, nc.sync)
+        load_pairs(0)
+        load_pairs(1)
         for q in range(4):
-            load_scales(nc.sync, c_plane, c_scales_v, q)
-            load_scales(nc.scalar, b_plane, b_scales_v, q)
-        load_codes(0, nc.gpsimd)
-        nc.gpsimd.dma_start(out=bias_rows[0:8, :], in_=pair_bias.rearrange("(c n) -> c n", n=256))
+            load_scales(nc.scalar, c_plane, c_scales_v, q)
+            load_scales(nc.gpsimd, b_plane, b_scales_v, q)
         for g in range(1, KG):
             load_codes(g, nc.sync)
         load_act(0)
         load_act(1)
         load_pairs(2)
         load_pairs(3)
-        load_act(2)
         load_pairs(4)
         load_pairs(5)
+        load_act(2)
         load_pairs(6)
-        load_act(3)
         load_pairs(7)
+        load_act(3)
+        for half in range(2):
+            cols = slice(1024 * half, 1024 * (half + 1))
+            nc.sync.dma_start(out=bias[:, cols], in_=pair_bias[cols].partition_broadcast(P))
         nc.scalar.activation(out=warm[:], in_=warm[:], func=ACT.Sigmoid)
-
-        def bias_step():
-            bank = new_bank()
-            nc.tensor.transpose(bank[:, 0:P], bias_rows[:].bitcast(F32), ident[:])
-            nc.scalar.copy(out=bias_cols[:], in_=bank[:, 0:8])
-            for half in range(2):
-                bank = new_bank()
-                for i in range(4):
-                    c = 4 * half + i
-                    nc.tensor.transpose(
-                        bank[:, i * P : (i + 1) * P], bias_cols[:, c : c + 1].to_broadcast([P, P]), ident[:]
-                    )
-                nc.scalar.copy(out=bias[:, 1024 * half : 1024 * (half + 1)].bitcast(F32), in_=bank[:])
 
         perm = {}
         grouped = {}
@@ -245,71 +231,70 @@ def tile_drug_synergy_bilinear_s4_kernel(
                 nc.sync.dma_start(out=out[P * m : P * (m + 1), 1024 * half : 1024 * (half + 1)], in_=z[:])
 
         pairs_permute(0)
+        pairs_permute(1)
         pairs_turn(0)
         pairs_turn(1)
-        pairs_permute(1)
         pairs_turn(2)
         pairs_turn(3)
         first_pair((0, 1))
         first(2)
-        bias_step()
         pairs_permute(2)
-        pairs_permute(3)
+        pairs_permute(3, nc.scalar.copy)
+        pairs_quantize(0, 0)
+        pairs_quantize(0, 1)
+        first(3)
         h_turn(0)
         h_turn(1)
         h_turn(2)
-        pairs_quantize(0, 0)
-        pairs_quantize(0, 1)
+        pairs_permute(4)
+        h_quantize(0)
         pairs_turn(4)
         pairs_turn(5)
-        first(3)
-        pairs_permute(4, nc.scalar.copy)
-        pairs_permute(5, nc.scalar.copy)
-        first(4)
         pairs_turn(6)
         pairs_turn(7)
-        pairs_permute(6)
-        pairs_permute(7)
+        h_turn(3)
+        pairs_permute(5, nc.scalar.copy)
         pairs_quantize(1, 0)
         pairs_quantize(1, 1)
-        h_quantize(0)
+        pairs_permute(6)
+        pairs_permute(7, nc.scalar.copy)
+        first(4)
         h_quantize(1)
+        h_quantize(2)
+        first(5)
         pairs_turn(8)
         pairs_turn(9)
         pairs_turn(10)
         pairs_turn(11)
         pairs_turn(12)
         pairs_turn(13)
-        pairs_quantize(2, 0)
-        pairs_quantize(2, 1)
         pairs_turn(14)
         pairs_turn(15)
-        h_quantize(2)
-        h_turn(3)
+        h_quantize(3)
         h_turn(4)
+        pairs_quantize(2, 0)
+        pairs_quantize(2, 1)
         second(0, 0)
-        first(5)
         pairs_quantize(3, 0)
         pairs_quantize(3, 1)
-        second(1, 0)
         first(6)
         second(0, 1)
-        second(1, 1)
-        h_quantize(3)
-        h_turn(5)
-        h_turn(6)
+        second(1, 0)
         h_quantize(4)
+        second(1, 1)
+        h_turn(5)
         second(2, 0)
         second(2, 1)
-        h_quantize(5)
         second(3, 0)
+        h_turn(6)
+        h_quantize(5)
         second(3, 1)
-        second(4, 0)
         first(7)
+        second(4, 0)
         second(4, 1)
         h_quantize(6)
-        h_turn(7)
         second(5, 0)
+        h_turn(7)
         second(5, 1)
         second(6, 0)
         h_quantize(7)

@@ -21,7 +21,6 @@ KG = K // 512
 FG = F // 512
 MT = M // P
 RT = R // P
-RC = R // 512
 
 
 def tile_drug_synergy_bilinear_s4_kernel(
@@ -30,7 +29,7 @@ def tile_drug_synergy_bilinear_s4_kernel(
     nc = tc.nc
     with ExitStack() as ctx:
         keep = ctx.enter_context(tc.tile_pool(name="keep", bufs=1))
-        work = ctx.enter_context(tc.tile_pool(name="work", bufs=3))
+        work = ctx.enter_context(tc.tile_pool(name="work", bufs=4))
         psum = ctx.enter_context(tc.psum_pool(name="psum", bufs=8))
         ctx.enter_context(tc.manual_schedule())
 
@@ -40,10 +39,10 @@ def tile_drug_synergy_bilinear_s4_kernel(
         def new_bank():
             return psum.tile([P, 512], F32, name="bank", tag="bank")
 
-        c_plane = fixed("c_plane", [P, KG * M], U8)
-        b_plane = fixed("b_plane", [P, KG * F], U8)
-        c_code = [fixed("c_code%d" % g, [P, 2 * M], U8) for g in range(KG)]
-        b_code = [fixed("b_code%d" % g, [P, 2 * F], U8) for g in range(KG)]
+        c_plane = [fixed("c_plane%d" % i, [P, KG, 512], U8) for i in range(2)]
+        b_plane = [fixed("b_plane%d" % i, [P, KG, 512], U8) for i in range(2)]
+        c_code = [[fixed("c_code%d%d" % (i, h), [P, 2, 1024], U8) for h in range(2)] for i in range(2)]
+        b_code = [[fixed("b_code%d%d" % (i, h), [P, 2, 1024], U8) for h in range(2)] for i in range(2)]
         act = [fixed("act%d" % j, [P, 2, F], BF16) for j in range(MT // 2)]
         raw = [fixed("raw%d" % j, [P, 2, F], BF16) for j in range(RT // 2)]
         d_code = fixed("d_code", [P, FG, R], U32)
@@ -52,13 +51,18 @@ def tile_drug_synergy_bilinear_s4_kernel(
         bias = fixed("bias", [P, R], BF16)
         warm = fixed("warm", [P, 1], F32)
 
-        nc.vector.memset(c_plane[:].bitcast(I32), 0)
-        nc.vector.memset(b_plane[:].bitcast(I32), 0)
+        def clear(engine, plane):
+            engine.memset(plane[:].rearrange("p g n -> p (g n)").bitcast(I32), 0)
+
+        clear(nc.vector, c_plane[0])
+        clear(nc.vector, b_plane[0])
         nc.vector.memset(warm[:], 0.0)
         pairs_v = pairs.rearrange("(n i p) k -> n p i k", i=2, p=P)
         act_v = activity.rearrange("(n i p) f -> n p i f", i=2, p=P)
         c_scales_v = c_scales.bitcast(I32).rearrange("g r n -> r g n")
         b_scales_v = b_scales.bitcast(I32).rearrange("g r n -> r g n")
+        c_words_v = c_words.bitcast(I32).rearrange("(h g) p n -> h p g n", g=2)
+        b_words_v = b_words.bitcast(I32).rearrange("(h g) p n -> h p g n", g=2)
 
         def load_pairs(j, queue=nc.sync):
             queue.dma_start(out=raw[j][:], in_=pairs_v[j])
@@ -66,33 +70,41 @@ def tile_drug_synergy_bilinear_s4_kernel(
         def load_act(j):
             nc.sync.dma_start(out=act[j][:], in_=act_v[j])
 
-        def load_codes(g, queue):
-            queue.dma_start(out=c_code[g][:].bitcast(I32), in_=c_words[g].bitcast(I32))
-            queue.dma_start(out=b_code[g][:].bitcast(I32), in_=b_words[g].bitcast(I32))
+        def load_codes(queue, codes, source, i, h):
+            queue.dma_start(out=codes[i][h][:].bitcast(I32), in_=source[h, :, :, 256 * i : 256 * (i + 1)])
 
-        def load_scales(queue, plane, source, q):
-            queue.dma_start(
-                out=plane[32 * q : 32 * q + 4, :].bitcast(I32).rearrange("p (g n) -> p g n", g=KG),
-                in_=source[4 * q : 4 * q + 4],
-            )
+        def load_scales(queue, plane, source, i):
+            for q in range(4):
+                queue.dma_start(
+                    out=plane[i][32 * q : 32 * q + 4].bitcast(I32),
+                    in_=source[4 * q : 4 * q + 4, :, 128 * i : 128 * (i + 1)],
+                )
 
-        make_identity(nc, ident[:])
-        load_codes(0, nc.sync)
         load_pairs(0)
+        load_codes(nc.gpsimd, c_code, c_words_v, 0, 0)
+        load_codes(nc.gpsimd, b_code, b_words_v, 0, 0)
+        make_identity(nc, ident[:])
+        clear(nc.gpsimd, b_plane[1])
+        clear(nc.gpsimd, c_plane[1])
+        load_scales(nc.scalar, c_plane, c_scales_v, 0)
+        load_scales(nc.sync, b_plane, b_scales_v, 0)
+        load_codes(nc.sync, c_code, c_words_v, 0, 1)
+        load_codes(nc.sync, b_code, b_words_v, 0, 1)
+        load_scales(nc.sync, b_plane, b_scales_v, 1)
+        load_codes(nc.sync, b_code, b_words_v, 1, 0)
+        load_codes(nc.sync, b_code, b_words_v, 1, 1)
         load_pairs(1)
-        for q in range(4):
-            load_scales(nc.scalar, c_plane, c_scales_v, q)
-            load_scales(nc.gpsimd, b_plane, b_scales_v, q)
-        for g in range(1, KG):
-            load_codes(g, nc.sync)
+        load_pairs(2)
         load_act(0)
         load_act(1)
-        load_pairs(2)
         load_pairs(3)
+        load_scales(nc.sync, c_plane, c_scales_v, 1)
+        load_codes(nc.sync, c_code, c_words_v, 1, 0)
+        load_codes(nc.sync, c_code, c_words_v, 1, 1)
         load_pairs(4)
         load_pairs(5)
-        load_act(2)
         load_pairs(6)
+        load_act(2)
         load_pairs(7)
         load_act(3)
         for half in range(2):
@@ -138,12 +150,14 @@ def tile_drug_synergy_bilinear_s4_kernel(
             )
 
         def first_pass(bank, m, f, g):
+            h, s = g // 2, g % 2
+            c_cols = slice(P * (m % 4), P * (m % 4 + 1))
             nc.tensor.matmul_mx(
                 out=bank[:],
-                lhsT=c_code[g][:, 256 * m : 256 * (m + 1)].bitcast(FP4X4),
-                lhsT_scale=c_plane[:, M * g + P * m : M * g + P * (m + 1)],
-                rhs=b_code[g][:, 1024 * f : 1024 * (f + 1)].bitcast(FP4X4),
-                rhs_scale=b_plane[:, F * g + 512 * f : F * g + 512 * (f + 1)],
+                lhsT=c_code[m // 4][h][:, s, 256 * (m % 4) : 256 * (m % 4 + 1)].bitcast(FP4X4),
+                lhsT_scale=c_plane[m // 4][:, g, c_cols],
+                rhs=b_code[f][h][:, s, :].bitcast(FP4X4),
+                rhs_scale=b_plane[f][:, g, :],
                 start=(g == 0),
                 stop=(g == KG - 1),
             )
@@ -155,7 +169,7 @@ def tile_drug_synergy_bilinear_s4_kernel(
 
         def gate(bank, m, f):
             if f == 0:
-                gated[m] = work.tile([P, F], BF16, name="gated", tag="gated", bufs=4, align_bytes=64)
+                gated[m] = work.tile([P, F], BF16, name="gated", tag="gated", bufs=6, align_bytes=64)
             nc.vector.tensor_tensor(
                 out=gated[m][:].rearrange("p (u g n) -> p u g n", u=2, g=FG)[:, :, f, :].rearrange("p u (b x) -> p u b x", x=16),
                 in0=bank[:].rearrange("p (b u x) -> p u b x", u=2, x=16),
@@ -163,25 +177,23 @@ def tile_drug_synergy_bilinear_s4_kernel(
                 op=ALU.mult,
             )
 
-        def first(m):
-            for f in range(2):
-                bank = new_bank()
-                for g in range(KG):
-                    first_pass(bank, m, f, g)
-                gate(bank, m, f)
-
-        def first_pair(ms):
-            banks = {}
-            for m in ms:
-                for f in range(2):
-                    banks[(m, f)] = new_bank()
+        def first_half(m, f):
+            bank = new_bank()
             for g in range(KG):
-                for m in ms:
-                    for f in range(2):
-                        first_pass(banks[(m, f)], m, f, g)
-            for m in ms:
-                for f in range(2):
-                    gate(banks[(m, f)], m, f)
+                first_pass(bank, m, f, g)
+            gate(bank, m, f)
+
+        four = []
+
+        def first_four(h):
+            if h == 0:
+                four.extend([new_bank() for m in range(4)])
+            for m in range(4):
+                for g in range(2 * h, 2 * h + 2):
+                    first_pass(four[m], m, 0, g)
+            if h == 1:
+                for m in range(4):
+                    gate(four[m], m, 0)
 
         def h_turn(m):
             bank = new_bank()
@@ -199,105 +211,116 @@ def tile_drug_synergy_bilinear_s4_kernel(
             )
 
         def h_quantize(m):
-            h_code[m] = work.tile([P, FG * P], U32, name="h_code", tag="h_code", bufs=4, align_bytes=64)
-            h_plane[m] = work.tile([P, FG * P], U8, name="h_plane", tag="h_plane", bufs=4, align_bytes=64)
+            h_code[m] = work.tile([P, FG * P], U32, name="h_code", tag="h_code", bufs=6, align_bytes=64)
+            h_plane[m] = work.tile([P, FG * P], U8, name="h_plane", tag="h_plane", bufs=6, align_bytes=64)
             nc.vector.quantize_mx(out=h_code[m][:].bitcast(FP8X4), scales=h_plane[m][:], in_=h_turned[m][:])
 
-        def second(m, half, fine=False):
-            z = work.tile([P, 1024], F32, name="z", tag="z", bufs=6, align_bytes=64)
+        def second(m, half, pieces=((0, 1024),)):
+            z = work.tile([P, 1024], F32, name="z", tag="z", bufs=8, align_bytes=64)
             for i in range(2):
-                rc = 2 * half + i
                 bank = new_bank()
-                cols = slice(512 * rc, 512 * (rc + 1))
+                d_cols = slice(1024 * half + 512 * i, 1024 * half + 512 * (i + 1))
                 for g in range(FG):
                     nc.tensor.matmul_mx(
                         out=bank[:],
                         lhsT=h_code[m][:, P * g : P * (g + 1)].bitcast(FP8X4),
                         lhsT_scale=h_plane[m][:, P * g : P * (g + 1)],
-                        rhs=d_code[:, g, cols].bitcast(FP8X4),
-                        rhs_scale=d_plane[:, g, cols],
+                        rhs=d_code[:, g, d_cols].bitcast(FP8X4),
+                        rhs_scale=d_plane[:, g, d_cols],
                         start=(g == 0),
                         stop=(g == FG - 1),
                     )
-                nc.vector.tensor_tensor(
-                    out=z[:, 512 * i : 512 * (i + 1)], in0=bank[:], in1=bias[:, cols], op=ALU.add
-                )
-                if fine:
-                    part = slice(512 * i, 512 * (i + 1))
-                    nc.scalar.activation(out=z[:, part], in_=z[:, part], func=ACT.Sigmoid)
-                    nc.sync.dma_start(out=out[P * m : P * (m + 1), cols], in_=z[:, part])
-            if not fine:
-                nc.scalar.activation(out=z[:], in_=z[:], func=ACT.Sigmoid)
-                nc.sync.dma_start(out=out[P * m : P * (m + 1), 1024 * half : 1024 * (half + 1)], in_=z[:])
+                for first_col, end_col in pieces:
+                    lo, hi = max(first_col, 512 * i), min(end_col, 512 * (i + 1))
+                    if lo < hi:
+                        nc.vector.tensor_tensor(
+                            out=z[:, lo:hi],
+                            in0=bank[:, lo - 512 * i : hi - 512 * i],
+                            in1=bias[:, 1024 * half + lo : 1024 * half + hi],
+                            op=ALU.add,
+                        )
+                    if lo < hi and hi == end_col:
+                        piece = z[:, first_col:end_col]
+                        nc.scalar.activation(out=piece, in_=piece, func=ACT.Sigmoid)
+                        nc.sync.dma_start(
+                            out=out[P * m : P * (m + 1), 1024 * half + first_col : 1024 * half + end_col], in_=piece
+                        )
 
         pairs_permute(0)
-        pairs_permute(1)
+        pairs_permute(1, nc.scalar.copy)
+        pairs_permute(2)
         pairs_turn(0)
         pairs_turn(1)
+        first_four(0)
+        first_four(1)
+        first_half(0, 1)
+        first_half(1, 1)
         pairs_turn(2)
         pairs_turn(3)
-        first_pair((0, 1))
-        first(2)
-        pairs_permute(2)
-        pairs_permute(3, nc.scalar.copy)
-        pairs_quantize(0, 0)
-        pairs_quantize(0, 1)
-        first(3)
-        h_turn(0)
-        h_turn(1)
-        h_turn(2)
-        pairs_permute(4)
-        h_quantize(0)
         pairs_turn(4)
         pairs_turn(5)
+        pairs_permute(3)
+        first_half(2, 1)
+        first_half(3, 1)
+        h_turn(0)
         pairs_turn(6)
         pairs_turn(7)
-        h_turn(3)
-        pairs_permute(5, nc.scalar.copy)
-        pairs_quantize(1, 0)
-        pairs_quantize(1, 1)
-        pairs_permute(6)
-        pairs_permute(7, nc.scalar.copy)
-        first(4)
+        h_turn(1)
+        h_quantize(0)
+        h_turn(2)
+        pairs_permute(4)
+        pairs_permute(5)
+        pairs_permute(6, nc.scalar.copy)
+        pairs_quantize(0, 0)
+        pairs_quantize(0, 1)
         h_quantize(1)
-        h_quantize(2)
-        first(5)
+        first_half(4, 0)
+        first_half(4, 1)
         pairs_turn(8)
         pairs_turn(9)
+        pairs_quantize(1, 0)
+        pairs_quantize(1, 1)
         pairs_turn(10)
         pairs_turn(11)
+        pairs_permute(7, nc.scalar.copy)
         pairs_turn(12)
         pairs_turn(13)
-        pairs_turn(14)
-        pairs_turn(15)
-        h_quantize(3)
-        h_turn(4)
         pairs_quantize(2, 0)
         pairs_quantize(2, 1)
-        second(0, 0)
+        first_half(5, 0)
+        first_half(5, 1)
+        pairs_turn(14)
+        pairs_turn(15)
+        h_quantize(2)
+        h_turn(3)
         pairs_quantize(3, 0)
         pairs_quantize(3, 1)
-        first(6)
-        second(0, 1)
-        second(1, 0)
-        h_quantize(4)
-        second(1, 1)
+        h_turn(4)
         h_turn(5)
-        second(2, 0)
-        second(2, 1)
-        second(3, 0)
-        h_turn(6)
+        h_quantize(3)
+        h_quantize(4)
+        second(0, 0)
+        first_half(6, 0)
+        first_half(6, 1)
+        second(1, 0)
         h_quantize(5)
-        second(3, 1)
-        first(7)
+        second(0, 1)
+        second(2, 0)
+        second(3, 0)
+        second(1, 1)
         second(4, 0)
-        second(4, 1)
-        h_quantize(6)
+        second(2, 1)
         second(5, 0)
+        h_turn(6)
+        second(3, 1)
+        first_half(7, 0)
+        first_half(7, 1)
+        h_quantize(6)
+        second(4, 1)
         h_turn(7)
-        second(5, 1)
-        second(6, 0)
+        second(6, 0, ((0, 512), (512, 1024)))
+        second(5, 1, ((0, 512), (512, 1024)))
         h_quantize(7)
-        second(6, 1)
-        second(7, 0)
-        second(7, 1, fine=True)
+        second(6, 1, ((0, 512), (512, 1024)))
+        second(7, 0, ((0, 512), (512, 1024)))
+        second(7, 1, ((0, 512), (512, 768), (768, 1024)))

@@ -21,6 +21,8 @@ KG = K // 512
 FG = F // 512
 MT = M // P
 RT = R // P
+RC = R // 512
+WARM_UP = 2
 
 
 def tile_drug_synergy_bilinear_s4_kernel(
@@ -45,15 +47,18 @@ def tile_drug_synergy_bilinear_s4_kernel(
         b_code = [[fixed("b_code%d%d" % (i, h), [P, 2, 1024], U8) for h in range(2)] for i in range(2)]
         act = [fixed("act%d" % j, [P, 2, F], BF16) for j in range(MT // 2)]
         raw = [fixed("raw%d" % j, [P, 2, F], BF16) for j in range(RT // 2)]
-        d_code = fixed("d_code", [P, FG, R], U32)
-        d_plane = fixed("d_plane", [P, FG, R], U8)
+        d_code = fixed("d_code", [P, RC, FG, 512], U32)
+        d_plane = fixed("d_plane", [P, RC, FG, 512], U8)
         ident = fixed("ident", [P, P], F32)
+        bias_rows = fixed("bias_rows", [P, 256], BF16)
+        bias_cols = fixed("bias_cols", [P, 8], F32)
         bias = fixed("bias", [P, R], BF16)
         warm = fixed("warm", [P, 1], F32)
 
         def clear(engine, plane):
             engine.memset(plane[:].rearrange("p g n -> p (g n)").bitcast(I32), 0)
 
+        nc.vector.memset(bias_rows[:].bitcast(I32), 0)
         clear(nc.vector, c_plane[0])
         clear(nc.vector, b_plane[0])
         nc.vector.memset(warm[:], 0.0)
@@ -80,37 +85,51 @@ def tile_drug_synergy_bilinear_s4_kernel(
                     in_=source[4 * q : 4 * q + 4, :, 128 * i : 128 * (i + 1)],
                 )
 
-        load_pairs(0)
-        load_codes(nc.gpsimd, c_code, c_words_v, 0, 0)
-        load_codes(nc.gpsimd, b_code, b_words_v, 0, 0)
         make_identity(nc, ident[:])
-        clear(nc.gpsimd, b_plane[1])
         clear(nc.gpsimd, c_plane[1])
-        load_scales(nc.scalar, c_plane, c_scales_v, 0)
+        clear(nc.gpsimd, b_plane[1])
+        load_codes(nc.sync, c_code, c_words_v, 0, 0)
+        nc.scalar.dma_start(out=bias_rows[0:8, :], in_=pair_bias.rearrange("(c n) -> c n", n=256))
+        load_scales(nc.sync, c_plane, c_scales_v, 0)
+        load_codes(nc.sync, b_code, b_words_v, 0, 0)
         load_scales(nc.sync, b_plane, b_scales_v, 0)
+        load_pairs(0)
         load_codes(nc.sync, c_code, c_words_v, 0, 1)
         load_codes(nc.sync, b_code, b_words_v, 0, 1)
         load_scales(nc.sync, b_plane, b_scales_v, 1)
         load_codes(nc.sync, b_code, b_words_v, 1, 0)
         load_codes(nc.sync, b_code, b_words_v, 1, 1)
-        load_pairs(1)
-        load_pairs(2)
         load_act(0)
         load_act(1)
-        load_pairs(3)
-        load_scales(nc.sync, c_plane, c_scales_v, 1)
-        load_codes(nc.sync, c_code, c_words_v, 1, 0)
-        load_codes(nc.sync, c_code, c_words_v, 1, 1)
-        load_pairs(4)
-        load_pairs(5)
-        load_pairs(6)
-        load_act(2)
-        load_pairs(7)
-        load_act(3)
-        for half in range(2):
-            cols = slice(1024 * half, 1024 * (half + 1))
-            nc.sync.dma_start(out=bias[:, cols], in_=pair_bias[cols].partition_broadcast(P))
+        load_pairs(1)
+        load_pairs(2)
         nc.scalar.activation(out=warm[:], in_=warm[:], func=ACT.Sigmoid)
+
+        def bias_step():
+            bank = new_bank()
+            nc.tensor.transpose(bank[:, 0:P], bias_rows[:].bitcast(F32), ident[:])
+            nc.scalar.copy(out=bias_cols[:], in_=bank[:, 0:8])
+            for half in range(2):
+                bank = new_bank()
+                for i in range(4):
+                    c = 4 * half + i
+                    nc.tensor.transpose(
+                        bank[:, i * P : (i + 1) * P], bias_cols[:, c : c + 1].to_broadcast([P, P]), ident[:]
+                    )
+                nc.scalar.copy(out=bias[:, 1024 * half : 1024 * (half + 1)].bitcast(F32), in_=bank[:])
+
+        def warm_up():
+            bank = new_bank()
+            for i in range(WARM_UP):
+                nc.tensor.matmul_mx(
+                    out=bank[:],
+                    lhsT=c_code[0][0][:, 0, 0:256].bitcast(FP4X4),
+                    lhsT_scale=c_plane[1][:, 1, 0:P],
+                    rhs=b_code[0][0][:, 0, :].bitcast(FP4X4),
+                    rhs_scale=c_plane[1][:, 0, :],
+                    start=(i == 0),
+                    stop=(i == WARM_UP - 1),
+                )
 
         perm = {}
         grouped = {}
@@ -141,12 +160,11 @@ def tile_drug_synergy_bilinear_s4_kernel(
                 in_=bank[:].rearrange("p (g u r) -> p g r u", g=FG, u=2),
             )
 
-        def pairs_quantize(rc, g):
-            cols = slice(512 * rc, 512 * (rc + 1))
+        def pairs_quantize(rc):
             nc.vector.quantize_mx(
-                out=d_code[:, g, cols].bitcast(FP8X4),
-                scales=d_plane[:, g, cols],
-                in_=grouped[rc][:, g].rearrange("p r t -> p (r t)"),
+                out=d_code[:, rc].rearrange("p g r -> p (g r)").bitcast(FP8X4),
+                scales=d_plane[:, rc].rearrange("p g r -> p (g r)"),
+                in_=grouped[rc][:].rearrange("p g r t -> p (g r t)"),
             )
 
         def first_pass(bank, m, f, g):
@@ -219,14 +237,14 @@ def tile_drug_synergy_bilinear_s4_kernel(
             z = work.tile([P, 1024], F32, name="z", tag="z", bufs=8, align_bytes=64)
             for i in range(2):
                 bank = new_bank()
-                d_cols = slice(1024 * half + 512 * i, 1024 * half + 512 * (i + 1))
+                rc = 2 * half + i
                 for g in range(FG):
                     nc.tensor.matmul_mx(
                         out=bank[:],
                         lhsT=h_code[m][:, P * g : P * (g + 1)].bitcast(FP8X4),
                         lhsT_scale=h_plane[m][:, P * g : P * (g + 1)],
-                        rhs=d_code[:, g, d_cols].bitcast(FP8X4),
-                        rhs_scale=d_plane[:, g, d_cols],
+                        rhs=d_code[:, rc, g].bitcast(FP8X4),
+                        rhs_scale=d_plane[:, rc, g],
                         start=(g == 0),
                         stop=(g == FG - 1),
                     )
@@ -246,80 +264,88 @@ def tile_drug_synergy_bilinear_s4_kernel(
                             out=out[P * m : P * (m + 1), 1024 * half + first_col : 1024 * half + end_col], in_=piece
                         )
 
-        pairs_permute(0)
-        pairs_permute(1, nc.scalar.copy)
-        pairs_permute(2)
-        pairs_turn(0)
-        pairs_turn(1)
+        bias_step()
+        warm_up()
+        load_scales(nc.sync, c_plane, c_scales_v, 1)
+        load_codes(nc.sync, c_code, c_words_v, 1, 0)
+        load_codes(nc.sync, c_code, c_words_v, 1, 1)
+        load_pairs(3)
+        load_pairs(4)
+        load_act(2)
+        load_pairs(5)
+        load_pairs(6)
+        load_pairs(7)
+        load_act(3)
+        pairs_permute(0, nc.scalar.copy)
         first_four(0)
         first_four(1)
         first_half(0, 1)
+        pairs_turn(0)
+        pairs_turn(1)
         first_half(1, 1)
+        first_half(2, 1)
+        pairs_permute(1, nc.scalar.copy)
+        pairs_permute(2)
+        h_turn(0)
         pairs_turn(2)
         pairs_turn(3)
+        h_quantize(0)
+        pairs_permute(3)
+        h_turn(1)
+        first_half(3, 1)
         pairs_turn(4)
         pairs_turn(5)
-        pairs_permute(3)
-        first_half(2, 1)
-        first_half(3, 1)
-        h_turn(0)
-        pairs_turn(6)
-        pairs_turn(7)
-        h_turn(1)
-        h_quantize(0)
+        h_quantize(1)
         h_turn(2)
         pairs_permute(4)
-        pairs_permute(5)
-        pairs_permute(6, nc.scalar.copy)
-        pairs_quantize(0, 0)
-        pairs_quantize(0, 1)
-        h_quantize(1)
-        first_half(4, 0)
-        first_half(4, 1)
-        pairs_turn(8)
-        pairs_turn(9)
-        pairs_quantize(1, 0)
-        pairs_quantize(1, 1)
-        pairs_turn(10)
-        pairs_turn(11)
-        pairs_permute(7, nc.scalar.copy)
-        pairs_turn(12)
-        pairs_turn(13)
-        pairs_quantize(2, 0)
-        pairs_quantize(2, 1)
-        first_half(5, 0)
-        first_half(5, 1)
-        pairs_turn(14)
-        pairs_turn(15)
+        pairs_quantize(0)
         h_quantize(2)
         h_turn(3)
-        pairs_quantize(3, 0)
-        pairs_quantize(3, 1)
-        h_turn(4)
-        h_turn(5)
+        pairs_permute(5)
         h_quantize(3)
+        first_half(4, 0)
+        first_half(4, 1)
+        pairs_turn(6)
+        pairs_turn(7)
+        pairs_permute(6, nc.scalar.copy)
+        pairs_permute(7, nc.scalar.copy)
+        pairs_quantize(1)
+        first_half(5, 0)
+        first_half(5, 1)
+        h_turn(4)
         h_quantize(4)
+        pairs_turn(8)
+        pairs_turn(9)
+        pairs_turn(10)
+        pairs_turn(11)
         second(0, 0)
+        second(1, 0)
+        pairs_turn(12)
+        pairs_turn(13)
+        pairs_quantize(2)
+        pairs_turn(14)
+        pairs_turn(15)
+        second(2, 0)
         first_half(6, 0)
         first_half(6, 1)
-        second(1, 0)
-        h_quantize(5)
-        second(0, 1)
-        second(2, 0)
         second(3, 0)
-        second(1, 1)
-        second(4, 0)
-        second(2, 1)
-        second(5, 0)
+        pairs_quantize(3)
+        h_turn(5)
         h_turn(6)
-        second(3, 1)
+        second(4, 0)
+        second(0, 1)
+        second(1, 1)
         first_half(7, 0)
         first_half(7, 1)
-        h_quantize(6)
-        second(4, 1)
+        second(2, 1)
+        h_quantize(5)
         h_turn(7)
-        second(6, 0, ((0, 512), (512, 1024)))
+        second(3, 1)
+        second(5, 0)
+        second(4, 1, ((0, 512), (512, 1024)))
+        h_quantize(6)
         second(5, 1, ((0, 512), (512, 1024)))
+        second(6, 0, ((0, 512), (512, 1024)))
         h_quantize(7)
         second(6, 1, ((0, 512), (512, 1024)))
         second(7, 0, ((0, 512), (512, 1024)))

from contextlib import ExitStack

import concourse.mybir as mybir
from concourse.masks import make_identity

M, K, F, R = 1024, 2048, 1024, 2048
FLOPS = 2 * M * K * F + 2 * M * F * R

F32 = mybir.dt.float32
BF16 = mybir.dt.bfloat16
I32 = mybir.dt.int32
U32 = mybir.dt.uint32
U8 = mybir.dt.uint8
FP4X4 = mybir.dt.float4_e2m1fn_x4
FP8X4 = mybir.dt.float8_e4m3fn_x4
ACT = mybir.ActivationFunctionType
ALU = mybir.AluOpType

P = 128
KG = K // 512
FG = F // 512
MT = M // P
RT = R // P
RC = R // 512
WARM_UP = 2


def tile_drug_synergy_bilinear_s4_kernel(
    tc, c_words, c_scales, b_words, b_scales, activity, pairs, pair_bias, out
):
    nc = tc.nc
    with ExitStack() as ctx:
        keep = ctx.enter_context(tc.tile_pool(name="keep", bufs=1))
        work = ctx.enter_context(tc.tile_pool(name="work", bufs=4))
        psum = ctx.enter_context(tc.psum_pool(name="psum", bufs=8))
        ctx.enter_context(tc.manual_schedule())

        def fixed(name, shape, dtype):
            return keep.tile(shape, dtype, name=name, tag=name, align_bytes=64)

        def new_bank():
            return psum.tile([P, 512], F32, name="bank", tag="bank")

        c_plane = [fixed("c_plane%d" % i, [P, KG, 512], U8) for i in range(2)]
        b_plane = [fixed("b_plane%d" % i, [P, KG, 512], U8) for i in range(2)]
        c_code = [[fixed("c_code%d%d" % (i, h), [P, 2, 1024], U8) for h in range(2)] for i in range(2)]
        b_code = [[fixed("b_code%d%d" % (i, h), [P, 2, 1024], U8) for h in range(2)] for i in range(2)]
        act = [fixed("act%d" % j, [P, 2, F], BF16) for j in range(MT // 2)]
        raw = [fixed("raw%d" % j, [P, 2, F], BF16) for j in range(RT // 2)]
        d_code = fixed("d_code", [P, RC, FG, 512], U32)
        d_plane = fixed("d_plane", [P, RC, FG, 512], U8)
        ident = fixed("ident", [P, P], F32)
        bias_rows = fixed("bias_rows", [P, 256], BF16)
        bias_cols = fixed("bias_cols", [P, 8], F32)
        bias = fixed("bias", [P, R], BF16)
        warm = fixed("warm", [P, 1], F32)

        def clear(engine, plane):
            engine.memset(plane[:].rearrange("p g n -> p (g n)").bitcast(I32), 0)

        nc.vector.memset(bias_rows[:].bitcast(I32), 0)
        clear(nc.vector, c_plane[0])
        clear(nc.vector, b_plane[0])
        nc.vector.memset(warm[:], 0.0)
        pairs_v = pairs.rearrange("(n i p) k -> n p i k", i=2, p=P)
        act_v = activity.rearrange("(n i p) f -> n p i f", i=2, p=P)
        c_scales_v = c_scales.bitcast(I32).rearrange("g r n -> r g n")
        b_scales_v = b_scales.bitcast(I32).rearrange("g r n -> r g n")
        c_words_v = c_words.bitcast(I32).rearrange("(h g) p n -> h p g n", g=2)
        b_words_v = b_words.bitcast(I32).rearrange("(h g) p n -> h p g n", g=2)

        def load_pairs(j, queue=nc.sync):
            queue.dma_start(out=raw[j][:], in_=pairs_v[j])

        def load_act(j):
            nc.sync.dma_start(out=act[j][:], in_=act_v[j])

        def load_codes(queue, codes, source, i, h):
            queue.dma_start(out=codes[i][h][:].bitcast(I32), in_=source[h, :, :, 256 * i : 256 * (i + 1)])

        def load_scales(queue, plane, source, i):
            for q in range(4):
                queue.dma_start(
                    out=plane[i][32 * q : 32 * q + 4].bitcast(I32),
                    in_=source[4 * q : 4 * q + 4, :, 128 * i : 128 * (i + 1)],
                )

        make_identity(nc, ident[:])
        clear(nc.gpsimd, c_plane[1])
        clear(nc.gpsimd, b_plane[1])
        load_codes(nc.sync, c_code, c_words_v, 0, 0)
        nc.scalar.dma_start(out=bias_rows[0:8, :], in_=pair_bias.rearrange("(c n) -> c n", n=256))
        load_scales(nc.sync, c_plane, c_scales_v, 0)
        load_codes(nc.sync, b_code, b_words_v, 0, 0)
        load_scales(nc.sync, b_plane, b_scales_v, 0)
        load_pairs(0)
        load_codes(nc.sync, c_code, c_words_v, 0, 1)
        load_codes(nc.sync, b_code, b_words_v, 0, 1)
        load_scales(nc.sync, b_plane, b_scales_v, 1)
        load_codes(nc.sync, b_code, b_words_v, 1, 0)
        load_codes(nc.sync, b_code, b_words_v, 1, 1)
        load_act(0)
        load_act(1)
        load_pairs(1)
        load_pairs(2)
        nc.scalar.activation(out=warm[:], in_=warm[:], func=ACT.Sigmoid)

        def bias_step():
            bank = new_bank()
            nc.tensor.transpose(bank[:, 0:P], bias_rows[:].bitcast(F32), ident[:])
            nc.scalar.copy(out=bias_cols[:], in_=bank[:, 0:8])
            for half in range(2):
                bank = new_bank()
                for i in range(4):
                    c = 4 * half + i
                    nc.tensor.transpose(
                        bank[:, i * P : (i + 1) * P], bias_cols[:, c : c + 1].to_broadcast([P, P]), ident[:]
                    )
                nc.scalar.copy(out=bias[:, 1024 * half : 1024 * (half + 1)].bitcast(F32), in_=bank[:])

        def warm_up():
            bank = new_bank()
            for i in range(WARM_UP):
                nc.tensor.matmul_mx(
                    out=bank[:],
                    lhsT=c_code[0][0][:, 0, 0:256].bitcast(FP4X4),
                    lhsT_scale=c_plane[1][:, 1, 0:P],
                    rhs=b_code[0][0][:, 0, :].bitcast(FP4X4),
                    rhs_scale=c_plane[1][:, 0, :],
                    start=(i == 0),
                    stop=(i == WARM_UP - 1),
                )

        perm = {}
        grouped = {}

        def pairs_permute(j, copy=nc.vector.tensor_copy):
            t = work.tile([P, 2 * F // 2], F32, name="perm", tag="perm", bufs=4, align_bytes=64)
            perm[j] = t
            copy(
                out=t[:].rearrange("p (u n x) -> p u n x", u=2, x=8),
                in_=raw[j][:].rearrange("p i k -> p (i k)").bitcast(F32).rearrange("p (n u x) -> p u n x", u=2, x=8),
            )

        def pairs_turn(i):
            j, rc = i // 2, i // 4
            if i % 4 == 0:
                grouped[rc] = work.tile([P, FG, 512, 4], BF16, name="grouped", tag="grouped", bufs=2, align_bytes=64)
            bank = new_bank()
            words = perm[j][:]
            for g in range(FG):
                for u in range(2):
                    start = 512 * u + 256 * (i % 2) + 128 * g
                    nc.tensor.transpose(
                        bank[:, (2 * g + u) * P : (2 * g + u + 1) * P], words[:, start : start + P], ident[:]
                    )
            r0 = 128 * (i % 4)
            nc.scalar.copy(
                out=grouped[rc][:].rearrange("p g r t -> p g (r t)").bitcast(F32)[:, :, 2 * r0 : 2 * r0 + 256].rearrange("p g (r u) -> p g r u", u=2),
                in_=bank[:].rearrange("p (g u r) -> p g r u", g=FG, u=2),
            )

        def pairs_quantize(rc):
            nc.vector.quantize_mx(
                out=d_code[:, rc].rearrange("p g r -> p (g r)").bitcast(FP8X4),
                scales=d_plane[:, rc].rearrange("p g r -> p (g r)"),
                in_=grouped[rc][:].rearrange("p g r t -> p (g r t)"),
            )

        def first_pass(bank, m, f, g):
            h, s = g // 2, g % 2
            c_cols = slice(P * (m % 4), P * (m % 4 + 1))
            nc.tensor.matmul_mx(
                out=bank[:],
                lhsT=c_code[m // 4][h][:, s, 256 * (m % 4) : 256 * (m % 4 + 1)].bitcast(FP4X4),
                lhsT_scale=c_plane[m // 4][:, g, c_cols],
                rhs=b_code[f][h][:, s, :].bitcast(FP4X4),
                rhs_scale=b_plane[f][:, g, :],
                start=(g == 0),
                stop=(g == KG - 1),
            )

        gated = {}
        h_code = {}
        h_plane = {}
        h_turned = {}

        def gate(bank, m, f):
            if f == 0:
                gated[m] = work.tile([P, F], BF16, name="gated", tag="gated", bufs=6, align_bytes=64)
            nc.vector.tensor_tensor(
                out=gated[m][:].rearrange("p (u g n) -> p u g n", u=2, g=FG)[:, :, f, :].rearrange("p u (b x) -> p u b x", x=16),
                in0=bank[:].rearrange("p (b u x) -> p u b x", u=2, x=16),
                in1=act[m // 2][:, m % 2, 512 * f : 512 * (f + 1)].rearrange("p (b u x) -> p u b x", u=2, x=16),
                op=ALU.mult,
            )

        def first_half(m, f):
            bank = new_bank()
            for g in range(KG):
                first_pass(bank, m, f, g)
            gate(bank, m, f)

        four = []

        def first_four(h):
            if h == 0:
                four.extend([new_bank() for m in range(4)])
            for m in range(4):
                for g in range(2 * h, 2 * h + 2):
                    first_pass(four[m], m, 0, g)
            if h == 1:
                for m in range(4):
                    gate(four[m], m, 0)

        def h_turn(m):
            bank = new_bank()
            words = gated[m][:].bitcast(F32)
            for g in range(FG):
                for u in range(2):
                    start = 256 * u + 128 * g
                    nc.tensor.transpose(
                        bank[:, (2 * g + u) * P : (2 * g + u + 1) * P], words[:, start : start + P], ident[:]
                    )
            h_turned[m] = work.tile([P, 4 * FG * P], BF16, name="h_turned", tag="h_turned", bufs=4, align_bytes=64)
            nc.scalar.copy(
                out=h_turned[m][:].bitcast(F32).rearrange("p (g r u) -> p g r u", g=FG, u=2),
                in_=bank[:].rearrange("p (g u r) -> p g r u", g=FG, u=2),
            )

        def h_quantize(m):
            h_code[m] = work.tile([P, FG * P], U32, name="h_code", tag="h_code", bufs=6, align_bytes=64)
            h_plane[m] = work.tile([P, FG * P], U8, name="h_plane", tag="h_plane", bufs=6, align_bytes=64)
            nc.vector.quantize_mx(out=h_code[m][:].bitcast(FP8X4), scales=h_plane[m][:], in_=h_turned[m][:])

        def second(m, half, pieces=((0, 1024),)):
            z = work.tile([P, 1024], F32, name="z", tag="z", bufs=8, align_bytes=64)
            for i in range(2):
                bank = new_bank()
                rc = 2 * half + i
                for g in range(FG):
                    nc.tensor.matmul_mx(
                        out=bank[:],
                        lhsT=h_code[m][:, P * g : P * (g + 1)].bitcast(FP8X4),
                        lhsT_scale=h_plane[m][:, P * g : P * (g + 1)],
                        rhs=d_code[:, rc, g].bitcast(FP8X4),
                        rhs_scale=d_plane[:, rc, g],
                        start=(g == 0),
                        stop=(g == FG - 1),
                    )
                for first_col, end_col in pieces:
                    lo, hi = max(first_col, 512 * i), min(end_col, 512 * (i + 1))
                    if lo < hi:
                        nc.vector.tensor_tensor(
                            out=z[:, lo:hi],
                            in0=bank[:, lo - 512 * i : hi - 512 * i],
                            in1=bias[:, 1024 * half + lo : 1024 * half + hi],
                            op=ALU.add,
                        )
                    if lo < hi and hi == end_col:
                        piece = z[:, first_col:end_col]
                        nc.scalar.activation(out=piece, in_=piece, func=ACT.Sigmoid)
                        nc.sync.dma_start(
                            out=out[P * m : P * (m + 1), 1024 * half + first_col : 1024 * half + end_col], in_=piece
                        )

        bias_step()
        warm_up()
        load_scales(nc.sync, c_plane, c_scales_v, 1)
        load_codes(nc.sync, c_code, c_words_v, 1, 0)
        load_codes(nc.sync, c_code, c_words_v, 1, 1)
        load_pairs(3)
        load_pairs(4)
        load_act(2)
        load_pairs(5)
        load_pairs(6)
        load_pairs(7)
        load_act(3)
        pairs_permute(0, nc.scalar.copy)
        first_four(0)
        first_four(1)
        first_half(0, 1)
        pairs_turn(0)
        pairs_turn(1)
        first_half(1, 1)
        first_half(2, 1)
        pairs_permute(1, nc.scalar.copy)
        pairs_permute(2)
        h_turn(0)
        pairs_turn(2)
        pairs_turn(3)
        h_quantize(0)
        pairs_permute(3)
        h_turn(1)
        first_half(3, 1)
        pairs_turn(4)
        pairs_turn(5)
        h_quantize(1)
        h_turn(2)
        pairs_permute(4)
        pairs_quantize(0)
        h_quantize(2)
        h_turn(3)
        pairs_permute(5)
        h_quantize(3)
        first_half(4, 0)
        first_half(4, 1)
        pairs_turn(6)
        pairs_turn(7)
        pairs_permute(6, nc.scalar.copy)
        pairs_permute(7, nc.scalar.copy)
        pairs_quantize(1)
        first_half(5, 0)
        first_half(5, 1)
        h_turn(4)
        h_quantize(4)
        pairs_turn(8)
        pairs_turn(9)
        pairs_turn(10)
        pairs_turn(11)
        second(0, 0)
        second(1, 0)
        pairs_turn(12)
        pairs_turn(13)
        pairs_quantize(2)
        pairs_turn(14)
        pairs_turn(15)
        second(2, 0)
        first_half(6, 0)
        first_half(6, 1)
        second(3, 0)
        pairs_quantize(3)
        h_turn(5)
        h_turn(6)
        second(4, 0)
        second(0, 1)
        second(1, 1)
        first_half(7, 0)
        first_half(7, 1)
        second(2, 1)
        h_quantize(5)
        h_turn(7)
        second(3, 1)
        second(5, 0)
        second(4, 1, ((0, 512), (512, 1024)))
        h_quantize(6)
        second(5, 1, ((0, 512), (512, 1024)))
        second(6, 0, ((0, 512), (512, 1024)))
        h_quantize(7)
        second(6, 1, ((0, 512), (512, 1024)))
        second(7, 0, ((0, 512), (512, 1024)))
        second(7, 1, ((0, 512), (512, 768), (768, 1024)))
